import numpy as np
import ml_dtypes


def mxq(x, axis, fmt="e4m3"):
    dtype, down = {"e4m3": (ml_dtypes.float8_e4m3fn, 7), "e5m2": (ml_dtypes.float8_e5m2, 14)}[fmt]
    v = np.moveaxis(np.asarray(x, np.float32).astype(ml_dtypes.bfloat16).astype(np.float64), axis, -1)
    blocks = v.reshape(v.shape[:-1] + (-1, 32))
    amax = np.abs(blocks).max(-1, keepdims=True)
    byte = np.maximum(np.where(amax > 0, np.frexp(amax)[1] - 1 + 127, 0) - down, 1)
    scale = np.exp2(byte - 127.0)
    codes = (blocks / scale).astype(np.float32).astype(dtype).astype(np.float64)
    return np.moveaxis((codes * scale).reshape(v.shape), -1, axis)


WIDE = False


def mx_kscale(k):
    if not WIDE:
        return np.ones(k)
    levels = np.array([10, -10, 5, -5, 0])
    if k % 512:
        return np.exp2(np.random.permutation(np.resize(levels, k // 32))).repeat(32)
    a = np.empty((k // 512, 16))
    for p in range(k // 512):
        a[p, :8] = np.random.permutation(np.resize(levels, 8))
        for g in range(8):
            far = levels[np.abs(levels - a[p, g]) >= 10]
            a[p, g + 8] = far[np.random.randint(len(far))]
    return np.exp2(a.ravel()).repeat(32)


BF16 = ml_dtypes.bfloat16


def bf(x):
    return np.asarray(x, np.float32).astype(BF16)


def f64(x):
    return np.asarray(x).astype(np.float64)


T, D, E, R, F = 4096, 1024, 2, 512, 128


def expert_scores(a):
    return np.sqrt(np.sum(a * a, axis=-1))


def silu(v):
    return v / (1.0 + np.exp(-v))


def softmax_experts(score):
    e = np.exp(score - score.max(axis=0, keepdims=True))
    return e / e.sum(axis=0, keepdims=True)


def draw0():
    s, t = mx_kscale(D), mx_kscale(R)
    return {"x": bf(np.random.standard_normal((T, D)) * s),
            "wdown": bf(np.random.standard_normal((E, D, R)) / np.sqrt(D) / s[None, :, None]),
            "rgain": bf((1.0 + 0.1 * np.random.standard_normal((E, R))) * t),
            "wup": bf(np.random.standard_normal((E, R, F)) * 1.5 / np.sqrt(R) / t[None, :, None]),
            "wp": bf(np.random.standard_normal((E, D, F)) / np.sqrt(D) / s[None, :, None])}


def core(x, wdown, rgain, wup, wp):
    xq = mxq(f64(x), 1, "e4m3")
    a = xq @ mxq(f64(wdown), 1, "e4m3")
    score = expert_scores(a)
    g = softmax_experts(score)
    b = a * f64(rgain)[:, None, :]
    u = mxq(b, 2, "e4m3") @ mxq(f64(wup), 1, "e4m3")
    p = xq @ mxq(f64(wp), 1, "e4m3")
    return np.sum(g[:, :, None] * silu(u) * p, axis=0)


def e4m3fn_bytes(y):
    return np.clip(np.asarray(y, np.float64), -448.0, 448.0).astype(np.float32).astype(ml_dtypes.float8_e4m3fn).view(np.uint8)


def e4m3fn_values(b):
    return np.asarray(b, np.uint8).view(ml_dtypes.float8_e4m3fn).astype(np.float64)


def setup_inputs():
    d = draw0()
    x0 = np.asarray(d['x']).astype(np.float64)
    s = (np.max(np.abs(x0), axis=(0,), keepdims=True) / 448.0).astype(np.float32)
    out = {}
    for k, v in d.items():
        if k == 'x':
            out['x_bytes'] = e4m3fn_bytes(x0 / s.astype(np.float64))
            out['x_scale'] = s
        else:
            out[k] = v
    return out


def reference(x_bytes, x_scale, wdown, rgain, wup, wp):
    return core(e4m3fn_values(x_bytes) * x_scale.astype(np.float64), wdown, rgain, wup, wp)

@@ -1,0 +1,381 @@
+from contextlib import ExitStack
+
+import concourse.mybir as mybir
+from concourse.masks import make_identity
+
+T, D, E, R, F = 4096, 1024, 2, 512, 128
+P = 128
+PAIRS = T // (2 * P)
+TILES = 2 * PAIRS
+FLOPS = 2 * T * (D * E * R + D * E * F + E * R * F)
+
+F32 = mybir.dt.float32
+BF16 = mybir.dt.bfloat16
+I32 = mybir.dt.int32
+U32 = mybir.dt.uint32
+U8 = mybir.dt.uint8
+F8 = mybir.dt.float8_e4m3fn
+X4 = mybir.dt.float8_e4m3fn_x4
+ACT = mybir.ActivationFunctionType
+ALU = mybir.AluOpType
+
+SQRT_SEED = 532487669.0
+GROUPS = (4, 4, 4, 2, 2)
+AHEAD = 10
+
+
+def tile_autonomyofexpertsnormgate_t_kernel(tc, x_bytes, x_scale, wdown, rgain, wup, wp, out):
+    nc = tc.nc
+    with ExitStack() as ctx:
+        keep = ctx.enter_context(tc.tile_pool(name="keep", bufs=1))
+        stage = ctx.enter_context(tc.tile_pool(name="stage", bufs=2))
+        psum = ctx.enter_context(tc.psum_pool(name="psum", bufs=1))
+        ctx.enter_context(tc.manual_schedule())
+
+        xscale = keep.tile([P, D], F32, name="xscale")
+        nc.scalar.dma_start(out=xscale[:], in_=x_scale.rearrange("o k -> (o k)").partition_broadcast(P))
+        tiny = keep.tile([P, 1], F32, name="tiny")
+        nc.vector.memset(tiny[:], 0.0)
+        nc.scalar.activation(out=tiny[:], in_=tiny[:], func=ACT.Silu)
+        gain_raw = keep.tile([P, E * R], BF16, name="gain_raw")
+
+        xb = {}
+
+        def load_x(k):
+            xb_tile = stage.tile([P, 2, D], U8, name="xb", bufs=8)
+            xb[k] = xb_tile
+            nc.sync.dma_start(out=xb[k][:], in_=x_bytes[256 * k : 256 * k + 256, :].rearrange("(p m) d -> p m d", m=2))
+
+        wraw, wcode, wscale = {}, {}, {}
+
+        def load_w(e, g):
+            w_tile = keep.tile([P, 4, R], BF16, name="wraw%d%d" % (e, g))
+            wraw[e, g] = w_tile
+            nc.sync.dma_start(out=w_tile[:], in_=wdown[e, 512 * g : 512 * g + 512, :].rearrange("(p j) c -> p j c", j=4))
+
+        load_x(0)
+        load_w(0, 0)
+        load_w(0, 1)
+        load_x(1)
+        load_w(1, 0)
+        load_w(1, 1)
+        load_x(2)
+        nc.scalar.dma_start(out=gain_raw[:], in_=rgain.rearrange("e r -> (e r)").partition_broadcast(P))
+        load_x(3)
+        praw = keep.tile([P, E, 2, 4, F], BF16, name="praw")
+        for e in range(E):
+            nc.sync.dma_start(out=praw[:, e], in_=wp[e].rearrange("(g p j) f -> p g j f", g=2, j=4))
+        uraw = keep.tile([P, E, 4, F], BF16, name="uraw")
+        nc.sync.dma_start(out=uraw[:], in_=wup.rearrange("e (p j) f -> p e j f", j=4))
+        for k in range(4, PAIRS):
+            load_x(k)
+
+        ident = keep.tile([P, P], F32, name="ident")
+        make_identity(nc, ident[:])
+
+        gain = keep.tile([P, E, R], BF16, name="gain")
+        for e in range(E):
+            nc.gpsimd.tensor_copy(
+                out=gain[:, e, :].rearrange("q (u p i) -> q u p i", u=2, i=2),
+                in_=gain_raw[:, e * R : (e + 1) * R].rearrange("q (p u i) -> q u p i", u=2, i=2),
+            )
+
+        wgrp = {}
+
+        def group_w(eng, e, g, u):
+            if u == 0:
+                wg_tile = stage.tile([P, 4 * R], BF16, align_bytes=64, name="wgrp", bufs=2)
+                wgrp[e, g] = wg_tile
+            half = wgrp[e, g][:, 1024 * u : 1024 * (u + 1)].rearrange("q (p i j) -> q p i j", i=2, j=4)
+            src = wraw[e, g][:].rearrange("q j (p u i) -> q u p i j", u=2, i=2)[:, u]
+            if eng == "s":
+                nc.scalar.copy(out=half, in_=src)
+            else:
+                nc.vector.tensor_copy(out=half, in_=src)
+
+        def quant_w(e, g):
+            c_tile = keep.tile([P, R], U32, align_bytes=64, name="wcode%d%d" % (e, g))
+            s_tile = keep.tile([P, R], U8, align_bytes=64, name="wscale%d%d" % (e, g))
+            wcode[e, g], wscale[e, g] = c_tile, s_tile
+            nc.vector.quantize_mx(out=c_tile[:].bitcast(X4), scales=s_tile[:], in_=wgrp[e, g][:])
+
+        pgrp = keep.tile([P, 2, 4 * E * F], BF16, align_bytes=64, name="pgrp")
+        pcode = keep.tile([P, 2, E * F], U32, align_bytes=64, name="pcode")
+        pscale = keep.tile([P, 2, E * F], U8, align_bytes=64, name="pscale")
+        ugrp = keep.tile([P, 4 * E * F], BF16, align_bytes=64, name="ugrp")
+        ucode = keep.tile([P, E * F], U32, align_bytes=64, name="ucode")
+        uscale = keep.tile([P, E * F], U8, align_bytes=64, name="uscale")
+
+        def group_p(g):
+            nc.scalar.copy(
+                out=pgrp[:, g, :].rearrange("q (e f j) -> q e f j", e=E, j=4),
+                in_=praw[:, :, g].rearrange("q e j f -> q e f j"),
+            )
+
+        def quant_p(g):
+            nc.vector.quantize_mx(out=pcode[:, g, :].bitcast(X4), scales=pscale[:, g, :], in_=pgrp[:, g, :])
+
+        def group_u():
+            nc.scalar.copy(
+                out=ugrp[:].rearrange("q (e f j) -> q e f j", e=E, j=4),
+                in_=uraw[:].rearrange("q e j f -> q e f j"),
+            )
+
+        def quant_u():
+            nc.vector.quantize_mx(out=ucode[:].bitcast(X4), scales=uscale[:], in_=ugrp[:])
+
+        late = []
+
+        xs, xt, xg, xc, xsc = {}, {}, {}, {}, {}
+        acc, bb, bt, bg, bc, bsc = {}, {}, {}, {}, {}, {}
+        pps, ups, sil = {}, {}, {}
+        sumsq = keep.tile([P, TILES * E], F32, name="sumsq")
+        gate = keep.tile([P, TILES, E], F32, name="gate")
+
+        def scale_x(n):
+            xs_tile = stage.tile([P, D], BF16, align_bytes=64, name="xs", bufs=AHEAD + 2)
+            xs[n] = xs_tile
+            nc.vector.tensor_tensor(out=xs_tile[:], in0=xb[n // 2][:, n % 2, :].bitcast(F8), in1=xscale[:], op=ALU.mult)
+
+        def turn_x(n):
+            xt_tile = psum.tile([P, 2, 2, P], F32, name="xt")
+            xt[n] = xt_tile
+            words = xs[n][:].bitcast(F32)
+            for g in range(2):
+                for u in range(2):
+                    nc.tensor.transpose(xt_tile[:, g, u, :], words[:, 256 * g + u : 256 * (g + 1) : 2], ident[:])
+
+        def leave_x(n):
+            k, m = n // 2, n % 2
+            if m == 0:
+                xg_tile = stage.tile([P, 2 * D], BF16, align_bytes=64, name="xg", bufs=3)
+                xg[k] = xg_tile
+            nc.scalar.copy(
+                out=xg[k][:, D * m : D * (m + 1)].bitcast(F32).rearrange("q (g r u) -> q g r u", g=2, u=2),
+                in_=xt[n][:].rearrange("q g u r -> q g r u"),
+            )
+
+        def quant_x(k):
+            c_tile = keep.tile([P, 4 * P], U32, align_bytes=64, name="xc%d" % k)
+            s_tile = keep.tile([P, 4 * P], U8, align_bytes=64, name="xsc%d" % k)
+            xc[k], xsc[k] = c_tile, s_tile
+            nc.vector.quantize_mx(out=c_tile[:].bitcast(X4), scales=s_tile[:], in_=xg[k][:])
+
+        def mm_a(n, e):
+            k, m = n // 2, n % 2
+            a_tile = psum.tile([P, R], F32, name="acc%d" % ((2 * n + e) % 4))
+            acc[n, e] = a_tile
+            for g in range(2):
+                cols = slice((2 * m + g) * P, (2 * m + g + 1) * P)
+                nc.tensor.matmul_mx(
+                    out=a_tile[:],
+                    lhsT=xc[k][:, cols].bitcast(X4),
+                    lhsT_scale=xsc[k][:, cols],
+                    rhs=wcode[e, g][:].bitcast(X4),
+                    rhs_scale=wscale[e, g][:],
+                    start=(g == 0),
+                    stop=(g == 1),
+                )
+
+        def gain_b(n, e):
+            if e == 0:
+                bb_tile = stage.tile([P, E * R], BF16, align_bytes=64, name="bb", bufs=3)
+                bb[n] = bb_tile
+            nc.vector.tensor_tensor(out=bb[n][:, e * R : (e + 1) * R], in0=acc[n, e][:], in1=gain[:, e, :], op=ALU.mult)
+
+        def square(n, e):
+            junk = stage.tile([P, R], BF16, name="junk", bufs=2)
+            nc.scalar.activation(out=junk[:], in_=acc[n, e][:], func=ACT.Square, accum_out=sumsq[:, 2 * n + e : 2 * n + e + 1])
+
+        def turn_b(n):
+            bt_tile = psum.tile([P, E, 2, P], F32, name="bt")
+            bt[n] = bt_tile
+            words = bb[n][:].bitcast(F32)
+            for e in range(E):
+                for u in range(2):
+                    nc.tensor.transpose(bt_tile[:, e, u, :], words[:, 256 * e + 128 * u : 256 * e + 128 * (u + 1)], ident[:])
+
+        def leave_b(n):
+            k, m = n // 2, n % 2
+            if m == 0:
+                bg_tile = stage.tile([P, 2 * E * R], BF16, align_bytes=64, name="bg", bufs=3)
+                bg[k] = bg_tile
+            nc.scalar.copy(
+                out=bg[k][:, E * R * m : E * R * (m + 1)].bitcast(F32).rearrange("q (e r u) -> q e r u", e=E, u=2),
+                in_=bt[n][:].rearrange("q e u r -> q e r u"),
+            )
+
+        def quant_b(k):
+            c_tile = keep.tile([P, 4 * P], U32, align_bytes=64, name="bc%d" % k)
+            s_tile = keep.tile([P, 4 * P], U8, align_bytes=64, name="bsc%d" % k)
+            bc[k], bsc[k] = c_tile, s_tile
+            nc.vector.quantize_mx(out=c_tile[:].bitcast(X4), scales=s_tile[:], in_=bg[k][:])
+
+        def mm_final(k):
+            p_tile = psum.tile([P, 2, E * F], F32, name="pp")
+            u_tile = psum.tile([P, 2, E, F], F32, name="uu")
+            pps[k], ups[k] = p_tile, u_tile
+            for m in range(2):
+                for e in range(E):
+                    cols = slice((2 * m + e) * P, (2 * m + e + 1) * P)
+                    ecols = slice(e * F, (e + 1) * F)
+                    nc.tensor.matmul_mx(
+                        out=u_tile[:, m, e, :],
+                        lhsT=bc[k][:, cols].bitcast(X4),
+                        lhsT_scale=bsc[k][:, cols],
+                        rhs=ucode[:, ecols].bitcast(X4),
+                        rhs_scale=uscale[:, ecols],
+                        start=True,
+                        stop=True,
+                    )
+            for m in range(2):
+                for g in range(2):
+                    cols = slice((2 * m + g) * P, (2 * m + g + 1) * P)
+                    nc.tensor.matmul_mx(
+                        out=p_tile[:, m, :],
+                        lhsT=xc[k][:, cols].bitcast(X4),
+                        lhsT_scale=xsc[k][:, cols],
+                        rhs=pcode[:, g, :].bitcast(X4),
+                        rhs_scale=pscale[:, g, :],
+                        start=(g == 0),
+                        stop=(g == 1),
+                    )
+
+        def silu(k):
+            s_tile = stage.tile([P, 2, E, F], F32, name="sil", bufs=2)
+            sil[k] = s_tile
+            nc.scalar.activation(out=s_tile[:], in_=ups[k][:], func=ACT.Silu)
+
+        def mix(k):
+            y = stage.tile([P, E, 2, F], F32, name="y", bufs=2)
+            o = stage.tile([P, 2, F], F32, name="o", bufs=3)
+            for e in range(E):
+                for m in range(2):
+                    nc.vector.scalar_tensor_tensor(
+                        out=y[:, e, m, :],
+                        in0=sil[k][:, m, e, :],
+                        scalar=gate[:, 2 * k + m, e : e + 1],
+                        in1=pps[k][:, m, e * F : (e + 1) * F],
+                        op0=ALU.mult,
+                        op1=ALU.mult,
+                    )
+            nc.vector.tensor_tensor(out=o[:], in0=y[:, 0], in1=y[:, 1], op=ALU.add)
+            nc.sync.dma_start(out=out[256 * k : 256 * k + 256, :].rearrange("(p m) f -> p m f", m=2), in_=o[:])
+
+        def gate_steps(first, count):
+            t0, nt = 2 * first, 2 * count
+            ss = sumsq[:, E * t0 : E * (t0 + nt)]
+            seed = stage.tile([P, E * nt], I32, name="seed", bufs=2)
+            state = {"y": seed[:].bitcast(F32)}
+
+            def start():
+                nc.vector.tensor_scalar(out=seed[:], in0=ss.bitcast(I32), scalar1=0.5, scalar2=SQRT_SEED, op0=ALU.mult, op1=ALU.add)
+
+            def recip():
+                r = stage.tile([P, E * nt], F32, name="newton_r", bufs=2)
+                state["r"] = r
+                nc.vector.reciprocal(out=r[:], in_=state["y"])
+
+            def divide():
+                t = stage.tile([P, E * nt], F32, name="newton_t", bufs=2)
+                state["t"] = t
+                nc.vector.scalar_tensor_tensor(out=t[:], in0=ss, scalar=0.5, in1=state["r"][:], op0=ALU.mult, op1=ALU.mult)
+
+            def average():
+                y = stage.tile([P, E * nt], F32, name="newton_y", bufs=2)
+                nc.vector.scalar_tensor_tensor(out=y[:], in0=state["y"], scalar=0.5, in1=state["t"][:], op0=ALU.mult, op1=ALU.add)
+                state["y"] = y[:]
+
+            def finish():
+                d = stage.tile([P, nt], F32, name="gate_d", bufs=2)
+                h = stage.tile([P, nt], F32, name="gate_h", bufs=2)
+                both = state["y"].rearrange("q (n e) -> q e n", e=E)
+                nc.vector.tensor_tensor(out=d[:], in0=both[:, 0], in1=both[:, 1], op=ALU.subtract)
+                late.append(lambda: squash(d, h))
+
+            def squash(d, h):
+                nc.scalar.activation(out=h[:], in_=d[:], func=ACT.Tanh, scale=0.5)
+                for e in range(E):
+                    nc.gpsimd.tensor_scalar(
+                        out=gate[:, t0 : t0 + nt, e],
+                        in0=h[:],
+                        scalar1=(0.5, -0.5)[e],
+                        scalar2=0.5,
+                        op0=ALU.mult,
+                        op1=ALU.add,
+                    )
+                ready.extend(range(first, first + count))
+
+            return [start] + [recip, divide, average] * 3 + [finish]
+
+        small = []
+        ready = []
+        final = []
+        bounds, total = {}, 0
+        for count in GROUPS:
+            bounds[2 * (total + count) - 1] = (total, count)
+            total += count
+
+        def weave(count):
+            for i in range(count):
+                if small:
+                    small.pop(0)()
+
+        done = 0
+        s = -AHEAD
+        while done < PAIRS:
+            busy = 0 <= s < TILES
+            rate = 1 if s < TILES else 3
+            if 0 <= s + 4 < TILES:
+                turn_x(s + 4)
+            if 0 <= s - 1 < TILES:
+                turn_b(s - 1)
+            if busy:
+                gain_b(s, 0)
+                weave(rate)
+                gain_b(s, 1)
+            weave(rate)
+            if 0 <= s + AHEAD < TILES:
+                scale_x(s + AHEAD)
+            weave(rate)
+            if final:
+                mix(final.pop(0))
+                done += 1
+            if busy:
+                square(s, 0)
+            if 0 <= s + 4 < TILES:
+                leave_x(s + 4)
+            if busy:
+                square(s, 1)
+            if 0 <= s - 1 < TILES:
+                leave_b(s - 1)
+            if late:
+                late.pop(0)()
+            w = s + AHEAD - 1
+            if 0 <= w < 8:
+                group_w("s", w // 4, w // 2 % 2, w % 2)
+                if w % 2 == 1:
+                    quant_w(w // 4, w // 2 % 2)
+            if s in (1, 2):
+                group_p(s - 1)
+            if s in (2, 3):
+                quant_p(s - 2)
+            if s == 3:
+                group_u()
+            if s == 4:
+                quant_u()
+            if s % 2 == 0 and 0 <= (s + 2) // 2 < PAIRS:
+                quant_x((s + 2) // 2)
+            if s % 2 == 1 and 0 <= (s - 3) // 2 < PAIRS:
+                quant_b((s - 3) // 2)
+            if 0 <= s + 1 < TILES:
+                mm_a(s + 1, 0)
+                mm_a(s + 1, 1)
+            if ready and ready[0] in bc:
+                k = ready.pop(0)
+                mm_final(k)
+                silu(k)
+                final.append(k)
+            if s in bounds:
+                small.extend(gate_steps(*bounds[s]))
+            s += 1

@@ -19,9 +19,21 @@ X4 = mybir.dt.float8_e4m3fn_x4
 ACT = mybir.ActivationFunctionType
 ALU = mybir.AluOpType
 
-SQRT_SEED = 532487669.0
-GROUPS = (4, 4, 4, 2, 2)
+RSQRT_SEED = 1597463007.0
+NEWT_V = 13
+GROUPS = (1, 3, 2, 2, 5, 3)
 AHEAD = 10
+PACE = 1.15
+FLAG = 9
+FEND = 11
+ADD_V = 11
+TURN = ("xt", 2, "bt", 1)
+SEED = 1
+LATE = 2
+WG = True
+LTX, LLX, LTB, LLB, LMA, LQX, LQB = 5, 4, 0, 1, 1, 2, 5
+STEP = ('N', 'G0', 'QW', 'S0', 'G1', 'QB', 'M0', 'S1', 'SX', 'MX', 'M1', 'MF', 'QX', 'LB', 'N', 'W', 'TX', 'SI', 'LX', 'LA', 'TB', 'N', 'AD')
+TAIL = ('MF', 'N', 'LB', 'N', 'N', 'AD', 'QB', 'SI', 'LA', 'N', 'TB', 'MX')
 
 
 def tile_autonomyofexpertsnormgate_t_kernel(tc, x_bytes, x_scale, wdown, rgain, wup, wp, out):
@@ -107,7 +119,7 @@ def tile_autonomyofexpertsnormgate_t_kernel(tc, x_bytes, x_scale, wdown, rgain, 
         uscale = keep.tile([P, E * F], U8, align_bytes=64, name="uscale")
 
         def group_p(g):
-            nc.scalar.copy(
+            (nc.gpsimd.tensor_copy if WG else nc.scalar.copy)(
                 out=pgrp[:, g, :].rearrange("q (e f j) -> q e f j", e=E, j=4),
                 in_=praw[:, :, g].rearrange("q e j f -> q e f j"),
             )
@@ -116,7 +128,7 @@ def tile_autonomyofexpertsnormgate_t_kernel(tc, x_bytes, x_scale, wdown, rgain, 
             nc.vector.quantize_mx(out=pcode[:, g, :].bitcast(X4), scales=pscale[:, g, :], in_=pgrp[:, g, :])
 
         def group_u():
-            nc.scalar.copy(
+            (nc.gpsimd.tensor_copy if WG else nc.scalar.copy)(
                 out=ugrp[:].rearrange("q (e f j) -> q e f j", e=E, j=4),
                 in_=uraw[:].rearrange("q e j f -> q e f j"),
             )
@@ -124,6 +136,8 @@ def tile_autonomyofexpertsnormgate_t_kernel(tc, x_bytes, x_scale, wdown, rgain, 
         def quant_u():
             nc.vector.quantize_mx(out=ucode[:].bitcast(X4), scales=uscale[:], in_=ugrp[:])
 
+        sums = []
+        clock = [0]
         late = []
 
         xs, xt, xg, xc, xsc = {}, {}, {}, {}, {}
@@ -138,7 +152,7 @@ def tile_autonomyofexpertsnormgate_t_kernel(tc, x_bytes, x_scale, wdown, rgain, 
             nc.vector.tensor_tensor(out=xs_tile[:], in0=xb[n // 2][:, n % 2, :].bitcast(F8), in1=xscale[:], op=ALU.mult)
 
         def turn_x(n):
-            xt_tile = psum.tile([P, 2, 2, P], F32, name="xt")
+            xt_tile = psum.tile([P, 2, 2, P], F32, name=TURN[0], bufs=TURN[1])
             xt[n] = xt_tile
             words = xs[n][:].bitcast(F32)
             for g in range(2):
@@ -163,7 +177,7 @@ def tile_autonomyofexpertsnormgate_t_kernel(tc, x_bytes, x_scale, wdown, rgain, 
 
         def mm_a(n, e):
             k, m = n // 2, n % 2
-            a_tile = psum.tile([P, R], F32, name="acc%d" % ((2 * n + e) % 4))
+            a_tile = psum.tile([P, R], F32, name="acc", bufs=8 - 2 - TURN[1] - (TURN[3] if TURN[0] != TURN[2] else 0))
             acc[n, e] = a_tile
             for g in range(2):
                 cols = slice((2 * m + g) * P, (2 * m + g + 1) * P)
@@ -188,7 +202,7 @@ def tile_autonomyofexpertsnormgate_t_kernel(tc, x_bytes, x_scale, wdown, rgain, 
             nc.scalar.activation(out=junk[:], in_=acc[n, e][:], func=ACT.Square, accum_out=sumsq[:, 2 * n + e : 2 * n + e + 1])
 
         def turn_b(n):
-            bt_tile = psum.tile([P, E, 2, P], F32, name="bt")
+            bt_tile = psum.tile([P, E, 2, P], F32, name=TURN[2], bufs=TURN[3])
             bt[n] = bt_tile
             words = bb[n][:].bitcast(F32)
             for e in range(E):
@@ -247,7 +261,7 @@ def tile_autonomyofexpertsnormgate_t_kernel(tc, x_bytes, x_scale, wdown, rgain, 
             nc.scalar.activation(out=s_tile[:], in_=ups[k][:], func=ACT.Silu)
 
         def mix(k):
-            y = stage.tile([P, E, 2, F], F32, name="y", bufs=2)
+            y = stage.tile([P, E, 2, F], F32, name="y", bufs=3)
             o = stage.tile([P, 2, F], F32, name="o", bufs=3)
             for e in range(E):
                 for m in range(2):
@@ -259,39 +273,49 @@ def tile_autonomyofexpertsnormgate_t_kernel(tc, x_bytes, x_scale, wdown, rgain, 
                         op0=ALU.mult,
                         op1=ALU.mult,
                     )
-            nc.vector.tensor_tensor(out=o[:], in0=y[:, 0], in1=y[:, 1], op=ALU.add)
-            nc.sync.dma_start(out=out[256 * k : 256 * k + 256, :].rearrange("(p m) f -> p m f", m=2), in_=o[:])
 
-        def gate_steps(first, count):
+            def add():
+                eng = nc.vector if k >= ADD_V else nc.gpsimd
+                eng.tensor_tensor(out=o[:], in0=y[:, 0], in1=y[:, 1], op=ALU.add)
+                nc.sync.dma_start(out=out[256 * k : 256 * k + 256, :].rearrange("(p m) f -> p m f", m=2), in_=o[:])
+
+            sums.append(add)
+
+        def gate_steps(first, count, eng):
             t0, nt = 2 * first, 2 * count
             ss = sumsq[:, E * t0 : E * (t0 + nt)]
             seed = stage.tile([P, E * nt], I32, name="seed", bufs=2)
             state = {"y": seed[:].bitcast(F32)}
 
             def start():
-                nc.vector.tensor_scalar(out=seed[:], in0=ss.bitcast(I32), scalar1=0.5, scalar2=SQRT_SEED, op0=ALU.mult, op1=ALU.add)
+                nc.vector.tensor_scalar(out=seed[:], in0=ss.bitcast(I32), scalar1=-0.5, scalar2=RSQRT_SEED, op0=ALU.mult, op1=ALU.add)
 
-            def recip():
-                r = stage.tile([P, E * nt], F32, name="newton_r", bufs=2)
-                state["r"] = r
-                nc.vector.reciprocal(out=r[:], in_=state["y"])
+            def by_s():
+                t = stage.tile([P, E * nt], F32, name="newton", bufs=6)
+                eng.tensor_tensor(out=t[:], in0=ss, in1=state["y"], op=ALU.mult)
+                state["t"] = t[:]
 
-            def divide():
-                t = stage.tile([P, E * nt], F32, name="newton_t", bufs=2)
-                state["t"] = t
-                nc.vector.scalar_tensor_tensor(out=t[:], in0=ss, scalar=0.5, in1=state["r"][:], op0=ALU.mult, op1=ALU.mult)
+            def by_y():
+                t = stage.tile([P, E * nt], F32, name="newton", bufs=6)
+                eng.tensor_tensor(out=t[:], in0=state["t"], in1=state["y"], op=ALU.mult)
+                state["t"] = t[:]
 
-            def average():
-                y = stage.tile([P, E * nt], F32, name="newton_y", bufs=2)
-                nc.vector.scalar_tensor_tensor(out=y[:], in0=state["y"], scalar=0.5, in1=state["t"][:], op0=ALU.mult, op1=ALU.add)
-                state["y"] = y[:]
+            def slope(first=False):
+                t = stage.tile([P, E * nt], F32, name="newton", bufs=6)
+                lift = 1.000876 if first else 1.0
+                eng.tensor_scalar(out=t[:], in0=state["t"], scalar1=-0.5 * lift, scalar2=1.5 * lift, op0=ALU.mult, op1=ALU.add)
+                state["t"] = t[:]
+
+            def step():
+                by_y()
+                state["y"] = state["t"]
 
             def finish():
                 d = stage.tile([P, nt], F32, name="gate_d", bufs=2)
                 h = stage.tile([P, nt], F32, name="gate_h", bufs=2)
-                both = state["y"].rearrange("q (n e) -> q e n", e=E)
-                nc.vector.tensor_tensor(out=d[:], in0=both[:, 0], in1=both[:, 1], op=ALU.subtract)
-                late.append(lambda: squash(d, h))
+                both = state["t"].rearrange("q (n e) -> q e n", e=E)
+                eng.tensor_tensor(out=d[:], in0=both[:, 0], in1=both[:, 1], op=ALU.subtract)
+                late.append((clock[0] + LATE, lambda: squash(d, h)))
 
             def squash(d, h):
                 nc.scalar.activation(out=h[:], in_=d[:], func=ACT.Tanh, scale=0.5)
@@ -306,8 +330,9 @@ def tile_autonomyofexpertsnormgate_t_kernel(tc, x_bytes, x_scale, wdown, rgain, 
                     )
                 ready.extend(range(first, first + count))
 
-            return [start] + [recip, divide, average] * 3 + [finish]
+            return [start, by_s, by_y, lambda: slope(True), step] + [by_s, by_y, slope, step] * 2 + [by_s, finish]
 
+        silus = []
         small = []
         ready = []
         final = []
@@ -323,59 +348,80 @@ def tile_autonomyofexpertsnormgate_t_kernel(tc, x_bytes, x_scale, wdown, rgain, 
 
         done = 0
         s = -AHEAD
+        waiting = []
         while done < PAIRS:
+            clock[0] = s
             busy = 0 <= s < TILES
-            rate = 1 if s < TILES else 3
-            if 0 <= s + 4 < TILES:
-                turn_x(s + 4)
-            if 0 <= s - 1 < TILES:
-                turn_b(s - 1)
-            if busy:
-                gain_b(s, 0)
-                weave(rate)
-                gain_b(s, 1)
-            weave(rate)
-            if 0 <= s + AHEAD < TILES:
-                scale_x(s + AHEAD)
-            weave(rate)
-            if final:
-                mix(final.pop(0))
-                done += 1
-            if busy:
-                square(s, 0)
-            if 0 <= s + 4 < TILES:
-                leave_x(s + 4)
-            if busy:
-                square(s, 1)
-            if 0 <= s - 1 < TILES:
-                leave_b(s - 1)
-            if late:
-                late.pop(0)()
-            w = s + AHEAD - 1
-            if 0 <= w < 8:
-                group_w("s", w // 4, w // 2 % 2, w % 2)
-                if w % 2 == 1:
-                    quant_w(w // 4, w // 2 % 2)
-            if s in (1, 2):
-                group_p(s - 1)
-            if s in (2, 3):
-                quant_p(s - 2)
-            if s == 3:
-                group_u()
-            if s == 4:
-                quant_u()
-            if s % 2 == 0 and 0 <= (s + 2) // 2 < PAIRS:
-                quant_x((s + 2) // 2)
-            if s % 2 == 1 and 0 <= (s - 3) // 2 < PAIRS:
-                quant_b((s - 3) // 2)
-            if 0 <= s + 1 < TILES:
-                mm_a(s + 1, 0)
-                mm_a(s + 1, 1)
-            if ready and ready[0] in bc:
-                k = ready.pop(0)
-                mm_final(k)
-                silu(k)
-                final.append(k)
+            for tok in (STEP if s < TILES else TAIL):
+                if tok == "TX" and 0 <= s + LTX < TILES:
+                    turn_x(s + LTX)
+                elif tok == "LX" and 0 <= s + LLX < TILES:
+                    leave_x(s + LLX)
+                elif tok == "TB" and 0 <= s - LTB < TILES:
+                    turn_b(s - LTB)
+                elif tok == "LB" and 0 <= s - LLB < TILES:
+                    leave_b(s - LLB)
+                elif tok == "G0" and busy:
+                    gain_b(s, 0)
+                elif tok == "G1" and busy:
+                    gain_b(s, 1)
+                elif tok == "S0" and busy:
+                    square(s, 0)
+                elif tok == "S1" and busy:
+                    square(s, 1)
+                elif tok == "M0" and 0 <= s + LMA < TILES:
+                    mm_a(s + LMA, 0)
+                elif tok == "M1" and 0 <= s + LMA < TILES:
+                    mm_a(s + LMA, 1)
+                elif tok == "SX" and len(xs) < TILES and (s < 0 or (len(xs) - AHEAD) * PACE <= s):
+                    scale_x(len(xs))
+                elif tok == "N":
+                    weave(1)
+                elif tok == "MX" and final:
+                    mix(final.pop(0))
+                    done += 1
+                elif tok == "AD" and sums:
+                    sums.pop(0)()
+                elif tok == "LA" and late and (s >= late[0][0] or s >= TILES):
+                    late.pop(0)[1]()
+                elif tok == "QX" and (s + LQX) % 2 == 0 and 0 <= (s + LQX) // 2 < PAIRS:
+                    quant_x((s + LQX) // 2)
+                elif tok == "QB" and (s - LQB) % 2 == 0 and 0 <= (s - LQB) // 2 < PAIRS:
+                    quant_b((s - LQB) // 2)
+                elif tok == "W":
+                    w = s + AHEAD - 1
+                    if 0 <= w < 8:
+                        group_w("s", w // 4, w // 2 % 2, w % 2)
+                        if w % 2 == 1:
+                            quant_w(w // 4, w // 2 % 2)
+                    if s in (1, 2):
+                        group_p(s - 1)
+                    if s == 3:
+                        group_u()
+                elif tok == "QW":
+                    if s in (4, 5):
+                        quant_p(s - 4)
+                    if s == 6:
+                        quant_u()
+                elif tok == "MF":
+                    if ready and ready[0] in bc and not final and (s >= 2 * ready[0] + FLAG or s >= TILES - FEND):
+                        k = ready.pop(0)
+                        mm_final(k)
+                        final.append(k)
+                        silus.append(k)
+                elif tok == "SI" and silus:
+                    silu(silus.pop(0))
             if s in bounds:
-                small.extend(gate_steps(*bounds[s]))
+                waiting.append((s + (SEED if bounds[s][0] < NEWT_V else 0), bounds[s]))
+            if waiting and waiting[0][0] <= s:
+                group = waiting.pop(0)[1]
+                on_v = group[0] >= NEWT_V
+                steps = gate_steps(*group, nc.vector if on_v else nc.gpsimd)
+                if on_v:
+                    small.extend(steps)
+                else:
+                    for one in steps:
+                        one()
             s += 1
+        while sums:
+            sums.pop(0)()

@@ -19,21 +19,22 @@ X4 = mybir.dt.float8_e4m3fn_x4
 ACT = mybir.ActivationFunctionType
 ALU = mybir.AluOpType
 
-RSQRT_SEED = 1597463007.0
-NEWT_V = 13
-GROUPS = (1, 3, 2, 2, 5, 3)
-AHEAD = 10
-PACE = 1.15
-FLAG = 9
-FEND = 11
-ADD_V = 11
-TURN = ("xt", 2, "bt", 1)
+SQRT_SEED = 532487669.0
+GROUPS = (2, 6, 4, 2, 2)
+AHEAD = 11
+PACE = 1.25
+FLAG = 14
+FEND = 4
+WENG = "ssssssss"
+WPER = 1
+WFROM = 2
+WLAG = 0
+TURN = ("xt", 2, "xt", 2)
 SEED = 1
-LATE = 2
-WG = True
+LATE = 1
 LTX, LLX, LTB, LLB, LMA, LQX, LQB = 5, 4, 0, 1, 1, 2, 5
-STEP = ('N', 'G0', 'QW', 'S0', 'G1', 'QB', 'M0', 'S1', 'SX', 'MX', 'M1', 'MF', 'QX', 'LB', 'N', 'W', 'TX', 'SI', 'LX', 'LA', 'TB', 'N', 'AD')
-TAIL = ('MF', 'N', 'LB', 'N', 'N', 'AD', 'QB', 'SI', 'LA', 'N', 'TB', 'MX')
+STEP = ('LX', 'M0', 'QW', 'N', 'QB', 'W', 'M1', 'G0', 'N', 'G1', 'LA', 'LB', 'S0', 'MX', 'MF', 'SI', 'N', 'S1', 'TX', 'QX', 'SX', 'WQ', 'TB', 'AD')
+TAIL = ('N', 'LA', 'N', 'LB', 'AD', 'N', 'MX', 'MF', 'SI', 'N', 'TB', 'QB')
 
 
 def tile_autonomyofexpertsnormgate_t_kernel(tc, x_bytes, x_scale, wdown, rgain, wup, wp, out):
@@ -49,7 +50,7 @@ def tile_autonomyofexpertsnormgate_t_kernel(tc, x_bytes, x_scale, wdown, rgain, 
         tiny = keep.tile([P, 1], F32, name="tiny")
         nc.vector.memset(tiny[:], 0.0)
         nc.scalar.activation(out=tiny[:], in_=tiny[:], func=ACT.Silu)
-        gain_raw = keep.tile([P, E * R], BF16, name="gain_raw")
+        gain = keep.tile([P, E, 2 * P, 2], BF16, name="gain")
 
         xb = {}
 
@@ -72,7 +73,7 @@ def tile_autonomyofexpertsnormgate_t_kernel(tc, x_bytes, x_scale, wdown, rgain, 
         load_w(1, 0)
         load_w(1, 1)
         load_x(2)
-        nc.scalar.dma_start(out=gain_raw[:], in_=rgain.rearrange("e r -> (e r)").partition_broadcast(P))
+        nc.scalar.dma_start(out=gain[:].rearrange("q e a i -> q (e a i)"), in_=rgain.rearrange("e r -> (e r)").partition_broadcast(P))
         load_x(3)
         praw = keep.tile([P, E, 2, 4, F], BF16, name="praw")
         for e in range(E):
@@ -85,23 +86,18 @@ def tile_autonomyofexpertsnormgate_t_kernel(tc, x_bytes, x_scale, wdown, rgain, 
         ident = keep.tile([P, P], F32, name="ident")
         make_identity(nc, ident[:])
 
-        gain = keep.tile([P, E, R], BF16, name="gain")
-        for e in range(E):
-            nc.gpsimd.tensor_copy(
-                out=gain[:, e, :].rearrange("q (u p i) -> q u p i", u=2, i=2),
-                in_=gain_raw[:, e * R : (e + 1) * R].rearrange("q (p u i) -> q u p i", u=2, i=2),
-            )
-
         wgrp = {}
 
         def group_w(eng, e, g, u):
             if u == 0:
-                wg_tile = stage.tile([P, 4 * R], BF16, align_bytes=64, name="wgrp", bufs=2)
+                wg_tile = stage.tile([P, 4 * R], BF16, align_bytes=64, name="wgrp", bufs=4)
                 wgrp[e, g] = wg_tile
             half = wgrp[e, g][:, 1024 * u : 1024 * (u + 1)].rearrange("q (p i j) -> q p i j", i=2, j=4)
             src = wraw[e, g][:].rearrange("q j (p u i) -> q u p i j", u=2, i=2)[:, u]
             if eng == "s":
                 nc.scalar.copy(out=half, in_=src)
+            elif eng == "g":
+                nc.gpsimd.tensor_copy(out=half, in_=src)
             else:
                 nc.vector.tensor_copy(out=half, in_=src)
 
@@ -119,7 +115,7 @@ def tile_autonomyofexpertsnormgate_t_kernel(tc, x_bytes, x_scale, wdown, rgain, 
         uscale = keep.tile([P, E * F], U8, align_bytes=64, name="uscale")
 
         def group_p(g):
-            (nc.gpsimd.tensor_copy if WG else nc.scalar.copy)(
+            nc.scalar.copy(
                 out=pgrp[:, g, :].rearrange("q (e f j) -> q e f j", e=E, j=4),
                 in_=praw[:, :, g].rearrange("q e j f -> q e f j"),
             )
@@ -128,7 +124,7 @@ def tile_autonomyofexpertsnormgate_t_kernel(tc, x_bytes, x_scale, wdown, rgain, 
             nc.vector.quantize_mx(out=pcode[:, g, :].bitcast(X4), scales=pscale[:, g, :], in_=pgrp[:, g, :])
 
         def group_u():
-            (nc.gpsimd.tensor_copy if WG else nc.scalar.copy)(
+            nc.scalar.copy(
                 out=ugrp[:].rearrange("q (e f j) -> q e f j", e=E, j=4),
                 in_=uraw[:].rearrange("q e j f -> q e f j"),
             )
@@ -195,7 +191,12 @@ def tile_autonomyofexpertsnormgate_t_kernel(tc, x_bytes, x_scale, wdown, rgain, 
             if e == 0:
                 bb_tile = stage.tile([P, E * R], BF16, align_bytes=64, name="bb", bufs=3)
                 bb[n] = bb_tile
-            nc.vector.tensor_tensor(out=bb[n][:, e * R : (e + 1) * R], in0=acc[n, e][:], in1=gain[:, e, :], op=ALU.mult)
+            nc.vector.tensor_tensor(
+                out=bb[n][:, e * R : (e + 1) * R].rearrange("q (u p i) -> q u p i", u=2, i=2),
+                in0=acc[n, e][:].rearrange("q (u p i) -> q u p i", u=2, i=2),
+                in1=gain[:, e].rearrange("q (p u) i -> q u p i", u=2),
+                op=ALU.mult,
+            )
 
         def square(n, e):
             junk = stage.tile([P, R], BF16, name="junk", bufs=2)
@@ -275,62 +276,49 @@ def tile_autonomyofexpertsnormgate_t_kernel(tc, x_bytes, x_scale, wdown, rgain, 
                     )
 
             def add():
-                eng = nc.vector if k >= ADD_V else nc.gpsimd
-                eng.tensor_tensor(out=o[:], in0=y[:, 0], in1=y[:, 1], op=ALU.add)
+                nc.vector.tensor_tensor(out=o[:], in0=y[:, 0], in1=y[:, 1], op=ALU.add)
                 nc.sync.dma_start(out=out[256 * k : 256 * k + 256, :].rearrange("(p m) f -> p m f", m=2), in_=o[:])
 
             sums.append(add)
 
-        def gate_steps(first, count, eng):
+        def gate_steps(first, count):
             t0, nt = 2 * first, 2 * count
             ss = sumsq[:, E * t0 : E * (t0 + nt)]
             seed = stage.tile([P, E * nt], I32, name="seed", bufs=2)
             state = {"y": seed[:].bitcast(F32)}
 
             def start():
-                nc.vector.tensor_scalar(out=seed[:], in0=ss.bitcast(I32), scalar1=-0.5, scalar2=RSQRT_SEED, op0=ALU.mult, op1=ALU.add)
+                nc.vector.tensor_scalar(out=seed[:], in0=ss.bitcast(I32), scalar1=0.5, scalar2=SQRT_SEED, op0=ALU.mult, op1=ALU.add)
 
-            def by_s():
-                t = stage.tile([P, E * nt], F32, name="newton", bufs=6)
-                eng.tensor_tensor(out=t[:], in0=ss, in1=state["y"], op=ALU.mult)
-                state["t"] = t[:]
+            def recip():
+                r = stage.tile([P, E * nt], F32, name="newton_r", bufs=2)
+                state["r"] = r
+                nc.vector.reciprocal(out=r[:], in_=state["y"])
 
-            def by_y():
-                t = stage.tile([P, E * nt], F32, name="newton", bufs=6)
-                eng.tensor_tensor(out=t[:], in0=state["t"], in1=state["y"], op=ALU.mult)
-                state["t"] = t[:]
+            def divide():
+                t = stage.tile([P, E * nt], F32, name="newton_t", bufs=2)
+                state["t"] = t
+                nc.vector.scalar_tensor_tensor(out=t[:], in0=ss, scalar=0.5, in1=state["r"][:], op0=ALU.mult, op1=ALU.mult)
 
-            def slope(first=False):
-                t = stage.tile([P, E * nt], F32, name="newton", bufs=6)
-                lift = 1.000876 if first else 1.0
-                eng.tensor_scalar(out=t[:], in0=state["t"], scalar1=-0.5 * lift, scalar2=1.5 * lift, op0=ALU.mult, op1=ALU.add)
-                state["t"] = t[:]
-
-            def step():
-                by_y()
-                state["y"] = state["t"]
+            def average():
+                y = stage.tile([P, E * nt], F32, name="newton_y", bufs=2)
+                nc.vector.scalar_tensor_tensor(out=y[:], in0=state["y"], scalar=0.5, in1=state["t"][:], op0=ALU.mult, op1=ALU.add)
+                state["y"] = y[:]
 
             def finish():
                 d = stage.tile([P, nt], F32, name="gate_d", bufs=2)
                 h = stage.tile([P, nt], F32, name="gate_h", bufs=2)
-                both = state["t"].rearrange("q (n e) -> q e n", e=E)
-                eng.tensor_tensor(out=d[:], in0=both[:, 0], in1=both[:, 1], op=ALU.subtract)
+                both = state["y"].rearrange("q (n e) -> q e n", e=E)
+                nc.vector.tensor_tensor(out=d[:], in0=both[:, 0], in1=both[:, 1], op=ALU.subtract)
                 late.append((clock[0] + LATE, lambda: squash(d, h)))
 
             def squash(d, h):
                 nc.scalar.activation(out=h[:], in_=d[:], func=ACT.Tanh, scale=0.5)
                 for e in range(E):
-                    nc.gpsimd.tensor_scalar(
-                        out=gate[:, t0 : t0 + nt, e],
-                        in0=h[:],
-                        scalar1=(0.5, -0.5)[e],
-                        scalar2=0.5,
-                        op0=ALU.mult,
-                        op1=ALU.add,
-                    )
+                    nc.scalar.activation(out=gate[:, t0 : t0 + nt, e], in_=h[:], func=ACT.Copy, scale=(0.5, -0.5)[e], bias=0.5)
                 ready.extend(range(first, first + count))
 
-            return [start, by_s, by_y, lambda: slope(True), step] + [by_s, by_y, slope, step] * 2 + [by_s, finish]
+            return [start] + [recip, divide, average] * 3 + [finish]
 
         silus = []
         small = []
@@ -389,10 +377,12 @@ def tile_autonomyofexpertsnormgate_t_kernel(tc, x_bytes, x_scale, wdown, rgain, 
                 elif tok == "QB" and (s - LQB) % 2 == 0 and 0 <= (s - LQB) // 2 < PAIRS:
                     quant_b((s - LQB) // 2)
                 elif tok == "W":
-                    w = s + AHEAD - 1
-                    if 0 <= w < 8:
-                        group_w("s", w // 4, w // 2 % 2, w % 2)
-                        if w % 2 == 1:
+                    for w in range(WPER * (s + AHEAD - WFROM), WPER * (s + AHEAD - WFROM + 1)):
+                        if 0 <= w < 8:
+                            group_w(WENG[w], w // 4, w // 2 % 2, w % 2)
+                elif tok == "WQ":
+                    for w in range(WPER * (s + AHEAD - WFROM - WLAG), WPER * (s + AHEAD - WFROM - WLAG + 1)):
+                        if 0 <= w < 8 and w % 2 == 1:
                             quant_w(w // 4, w // 2 % 2)
                     if s in (1, 2):
                         group_p(s - 1)
@@ -412,16 +402,9 @@ def tile_autonomyofexpertsnormgate_t_kernel(tc, x_bytes, x_scale, wdown, rgain, 
                 elif tok == "SI" and silus:
                     silu(silus.pop(0))
             if s in bounds:
-                waiting.append((s + (SEED if bounds[s][0] < NEWT_V else 0), bounds[s]))
+                waiting.append((s + SEED, bounds[s]))
             if waiting and waiting[0][0] <= s:
-                group = waiting.pop(0)[1]
-                on_v = group[0] >= NEWT_V
-                steps = gate_steps(*group, nc.vector if on_v else nc.gpsimd)
-                if on_v:
-                    small.extend(steps)
-                else:
-                    for one in steps:
-                        one()
+                small.extend(gate_steps(*waiting.pop(0)[1]))
             s += 1
         while sums:
             sums.pop(0)()

@@ -20,21 +20,24 @@ ACT = mybir.ActivationFunctionType
 ALU = mybir.AluOpType
 
 SQRT_SEED = 532487669.0
-GROUPS = (2, 6, 4, 2, 2)
-AHEAD = 11
+GROUPS = (9, 4, 3)
+AHEAD = 13
 PACE = 1.25
-FLAG = 14
-FEND = 4
-WENG = "ssssssss"
+FLAG = -1
+FEND = -2
+WENG = 'sssvssss'
 WPER = 1
-WFROM = 2
-WLAG = 0
-TURN = ("xt", 2, "xt", 2)
-SEED = 1
-LATE = 1
-LTX, LLX, LTB, LLB, LMA, LQX, LQB = 5, 4, 0, 1, 1, 2, 5
-STEP = ('LX', 'M0', 'QW', 'N', 'QB', 'W', 'M1', 'G0', 'N', 'G1', 'LA', 'LB', 'S0', 'MX', 'MF', 'SI', 'N', 'S1', 'TX', 'QX', 'SX', 'WQ', 'TB', 'AD')
-TAIL = ('N', 'LA', 'N', 'LB', 'AD', 'N', 'MX', 'MF', 'SI', 'N', 'TB', 'QB')
+WFROM = 1
+WLAG = 2
+TURN = ('xt', 2, 'xt', 2)
+SEED = 0
+LATE = 0
+LS = 15
+SINGLES = 1
+LTX, LLX, LTB, LLB, LMA, LQX, LQB = 7, 6, 1, 2, 1, 3, 6
+STEP = ('MF', 'W', 'N', 'QX', 'QW', 'WQ', 'SX', 'AD', 'QB', 'M0', 'LA', 'S0', 'MX', 'M1', 'S1', 'LX', 'LB', 'G0', 'N', 'N', 'G1', 'TX', 'SI', 'TB')
+LATEST = ('M1', 'S1', 'LX', 'N', 'QB', 'QW', 'WQ', 'TX', 'AD', 'QX', 'M0', 'N', 'SI', 'G1', 'MX', 'S0', 'LB', 'LA', 'SX', 'N', 'MF', 'G0', 'TB', 'W')
+TAIL = ('N', 'SI', 'LB', 'AD', 'N', 'MX', 'N', 'MF', 'LA', 'QB', 'N', 'TB')
 
 
 def tile_autonomyofexpertsnormgate_t_kernel(tc, x_bytes, x_scale, wdown, rgain, wup, wp, out):
@@ -45,17 +48,15 @@ def tile_autonomyofexpertsnormgate_t_kernel(tc, x_bytes, x_scale, wdown, rgain, 
         psum = ctx.enter_context(tc.psum_pool(name="psum", bufs=1))
         ctx.enter_context(tc.manual_schedule())
 
-        xscale = keep.tile([P, D], F32, name="xscale")
-        nc.scalar.dma_start(out=xscale[:], in_=x_scale.rearrange("o k -> (o k)").partition_broadcast(P))
+        xscale = keep.tile([P, 2, D], F32, name="xscale")
         tiny = keep.tile([P, 1], F32, name="tiny")
         nc.vector.memset(tiny[:], 0.0)
-        nc.scalar.activation(out=tiny[:], in_=tiny[:], func=ACT.Silu)
         gain = keep.tile([P, E, 2 * P, 2], BF16, name="gain")
 
         xb = {}
 
         def load_x(k):
-            xb_tile = stage.tile([P, 2, D], U8, name="xb", bufs=8)
+            xb_tile = stage.tile([P, 2, D], U8, name="xb", bufs=6)
             xb[k] = xb_tile
             nc.sync.dma_start(out=xb[k][:], in_=x_bytes[256 * k : 256 * k + 256, :].rearrange("(p m) d -> p m d", m=2))
 
@@ -66,13 +67,22 @@ def tile_autonomyofexpertsnormgate_t_kernel(tc, x_bytes, x_scale, wdown, rgain, 
             wraw[e, g] = w_tile
             nc.sync.dma_start(out=w_tile[:], in_=wdown[e, 512 * g : 512 * g + 512, :].rearrange("(p j) c -> p j c", j=4))
 
-        load_x(0)
+        first = stage.tile([P, 2, D], U8, name="xb", bufs=6)
+        xb[0] = first
+        tokens = x_bytes[0:256, :].rearrange("(p m) d -> p m d", m=2)
+        spread = x_scale.rearrange("o k -> (o k)")
+        nc.sync.dma_start(out=xscale[:, 0, 0:512], in_=spread[0:512].partition_broadcast(P))
+        nc.sync.dma_start(out=first[:, 0, :], in_=tokens[:, 0, :])
+        nc.sync.dma_start(out=xscale[:, 0, 512:1024], in_=spread[512:1024].partition_broadcast(P))
+        nc.sync.dma_start(out=first[:, 1, :], in_=tokens[:, 1, :])
+        nc.scalar.activation(out=tiny[:], in_=tiny[:], func=ACT.Silu)
+        nc.scalar.copy(out=xscale[:, 1, :], in_=xscale[:, 0, :])
         load_w(0, 0)
-        load_w(0, 1)
         load_x(1)
+        load_w(0, 1)
         load_w(1, 0)
-        load_w(1, 1)
         load_x(2)
+        load_w(1, 1)
         nc.scalar.dma_start(out=gain[:].rearrange("q e a i -> q (e a i)"), in_=rgain.rearrange("e r -> (e r)").partition_broadcast(P))
         load_x(3)
         praw = keep.tile([P, E, 2, 4, F], BF16, name="praw")
@@ -90,10 +100,10 @@ def tile_autonomyofexpertsnormgate_t_kernel(tc, x_bytes, x_scale, wdown, rgain, 
 
         def group_w(eng, e, g, u):
             if u == 0:
-                wg_tile = stage.tile([P, 4 * R], BF16, align_bytes=64, name="wgrp", bufs=4)
+                wg_tile = stage.tile([P, 4 * R], BF16, align_bytes=64, name="wgrp", bufs=2)
                 wgrp[e, g] = wg_tile
-            half = wgrp[e, g][:, 1024 * u : 1024 * (u + 1)].rearrange("q (p i j) -> q p i j", i=2, j=4)
-            src = wraw[e, g][:].rearrange("q j (p u i) -> q u p i j", u=2, i=2)[:, u]
+            half = wgrp[e, g][:, 1024 * u : 1024 * (u + 1)].rearrange("q (i p j) -> q i p j", i=2, j=4)
+            src = wraw[e, g][:].rearrange("q j (p t) -> q t p j", t=4)[:, 2 * u : 2 * u + 2]
             if eng == "s":
                 nc.scalar.copy(out=half, in_=src)
             elif eng == "g":
@@ -138,19 +148,36 @@ def tile_autonomyofexpertsnormgate_t_kernel(tc, x_bytes, x_scale, wdown, rgain, 
 
         xs, xt, xg, xc, xsc = {}, {}, {}, {}, {}
         acc, bb, bt, bg, bc, bsc = {}, {}, {}, {}, {}, {}
+        ACCS = 8 - 2 - TURN[1] - (TURN[3] if TURN[0] != TURN[2] else 0)
         pps, ups, sil = {}, {}, {}
         sumsq = keep.tile([P, TILES * E], F32, name="sumsq")
         gate = keep.tile([P, TILES, E], F32, name="gate")
 
         def scale_x(n):
-            xs_tile = stage.tile([P, D], BF16, align_bytes=64, name="xs", bufs=AHEAD + 2)
-            xs[n] = xs_tile
-            nc.vector.tensor_tensor(out=xs_tile[:], in0=xb[n // 2][:, n % 2, :].bitcast(F8), in1=xscale[:], op=ALU.mult)
+            k, m = n // 2, n % 2
+            if m == 0:
+                xs_tile = stage.tile([P, 2, D], BF16, align_bytes=64, name="xs", bufs=AHEAD // 2 + 2)
+                xs[k] = xs_tile
+            if n == 0:
+                for c in range(2):
+                    cols = slice(512 * c, 512 * (c + 1))
+                    nc.vector.tensor_tensor(out=xs[k][:, 0, cols], in0=xb[k][:, 0, cols].bitcast(F8), in1=xscale[:, 0, cols], op=ALU.mult)
+                return 1
+            if k < SINGLES:
+                nc.vector.tensor_tensor(out=xs[k][:, m, :], in0=xb[k][:, m, :].bitcast(F8), in1=xscale[:, 0, :], op=ALU.mult)
+                return 1
+            nc.vector.tensor_tensor(
+                out=xs[k][:].rearrange("q m d -> q (m d)"),
+                in0=xb[k][:].rearrange("q m d -> q (m d)").bitcast(F8),
+                in1=xscale[:].rearrange("q m d -> q (m d)"),
+                op=ALU.mult,
+            )
+            return 2
 
         def turn_x(n):
             xt_tile = psum.tile([P, 2, 2, P], F32, name=TURN[0], bufs=TURN[1])
             xt[n] = xt_tile
-            words = xs[n][:].bitcast(F32)
+            words = xs[n // 2][:, n % 2, :].bitcast(F32)
             for g in range(2):
                 for u in range(2):
                     nc.tensor.transpose(xt_tile[:, g, u, :], words[:, 256 * g + u : 256 * (g + 1) : 2], ident[:])
@@ -173,7 +200,7 @@ def tile_autonomyofexpertsnormgate_t_kernel(tc, x_bytes, x_scale, wdown, rgain, 
 
         def mm_a(n, e):
             k, m = n // 2, n % 2
-            a_tile = psum.tile([P, R], F32, name="acc", bufs=8 - 2 - TURN[1] - (TURN[3] if TURN[0] != TURN[2] else 0))
+            a_tile = psum.tile([P, R], F32, name="acc", bufs=ACCS)
             acc[n, e] = a_tile
             for g in range(2):
                 cols = slice((2 * m + g) * P, (2 * m + g + 1) * P)
@@ -188,15 +215,20 @@ def tile_autonomyofexpertsnormgate_t_kernel(tc, x_bytes, x_scale, wdown, rgain, 
                 )
 
         def gain_b(n, e):
-            if e == 0:
+            if n not in bb:
                 bb_tile = stage.tile([P, E * R], BF16, align_bytes=64, name="bb", bufs=3)
                 bb[n] = bb_tile
             nc.vector.tensor_tensor(
                 out=bb[n][:, e * R : (e + 1) * R].rearrange("q (u p i) -> q u p i", u=2, i=2),
-                in0=acc[n, e][:].rearrange("q (u p i) -> q u p i", u=2, i=2),
+                in0=acc[n, e][:].rearrange("q (u i p) -> q u p i", u=2, i=2),
                 in1=gain[:, e].rearrange("q (p u) i -> q u p i", u=2),
                 op=ALU.mult,
             )
+
+        def new_bg(k):
+            if k not in bg:
+                bg_tile = stage.tile([P, 2 * E * R], BF16, align_bytes=64, name="bg", bufs=3)
+                bg[k] = bg_tile
 
         def square(n, e):
             junk = stage.tile([P, R], BF16, name="junk", bufs=2)
@@ -212,12 +244,11 @@ def tile_autonomyofexpertsnormgate_t_kernel(tc, x_bytes, x_scale, wdown, rgain, 
 
         def leave_b(n):
             k, m = n // 2, n % 2
-            if m == 0:
-                bg_tile = stage.tile([P, 2 * E * R], BF16, align_bytes=64, name="bg", bufs=3)
-                bg[k] = bg_tile
+            ne = E
+            new_bg(k)
             nc.scalar.copy(
-                out=bg[k][:, E * R * m : E * R * (m + 1)].bitcast(F32).rearrange("q (e r u) -> q e r u", e=E, u=2),
-                in_=bt[n][:].rearrange("q e u r -> q e r u"),
+                out=bg[k][:, E * R * m : E * R * m + ne * R].bitcast(F32).rearrange("q (e r u) -> q e r u", e=ne, u=2),
+                in_=bt[n][:, 0:ne].rearrange("q e u r -> q e r u"),
             )
 
         def quant_b(k):
@@ -337,10 +368,11 @@ def tile_autonomyofexpertsnormgate_t_kernel(tc, x_bytes, x_scale, wdown, rgain, 
         done = 0
         s = -AHEAD
         waiting = []
+        scaled = 0
         while done < PAIRS:
             clock[0] = s
             busy = 0 <= s < TILES
-            for tok in (STEP if s < TILES else TAIL):
+            for tok in (TAIL if s >= TILES else LATEST if s >= LS else STEP):
                 if tok == "TX" and 0 <= s + LTX < TILES:
                     turn_x(s + LTX)
                 elif tok == "LX" and 0 <= s + LLX < TILES:
@@ -361,8 +393,8 @@ def tile_autonomyofexpertsnormgate_t_kernel(tc, x_bytes, x_scale, wdown, rgain, 
                     mm_a(s + LMA, 0)
                 elif tok == "M1" and 0 <= s + LMA < TILES:
                     mm_a(s + LMA, 1)
-                elif tok == "SX" and len(xs) < TILES and (s < 0 or (len(xs) - AHEAD) * PACE <= s):
-                    scale_x(len(xs))
+                elif tok == "SX" and scaled < TILES and (scaled - AHEAD <= s if s < 0 else (scaled - AHEAD) * PACE <= s):
+                    scaled += scale_x(scaled)
                 elif tok == "N":
                     weave(1)
                 elif tok == "MX" and final:

@@ -20,24 +20,24 @@ ACT = mybir.ActivationFunctionType
 ALU = mybir.AluOpType
 
 SQRT_SEED = 532487669.0
-GROUPS = (9, 4, 3)
-AHEAD = 13
-PACE = 1.25
-FLAG = -1
-FEND = -2
-WENG = 'sssvssss'
-WPER = 1
-WFROM = 1
+GROUPS = (7, 4, 3, 2)
+AHEAD = 9
+PACE = 1.0
+FLAG = 20
+FEND = 73
+WENG = 'vssssvss'
+WPER = 2
+WFROM = 2
 WLAG = 2
 TURN = ('xt', 2, 'xt', 2)
 SEED = 0
 LATE = 0
-LS = 15
-SINGLES = 1
-LTX, LLX, LTB, LLB, LMA, LQX, LQB = 7, 6, 1, 2, 1, 3, 6
-STEP = ('MF', 'W', 'N', 'QX', 'QW', 'WQ', 'SX', 'AD', 'QB', 'M0', 'LA', 'S0', 'MX', 'M1', 'S1', 'LX', 'LB', 'G0', 'N', 'N', 'G1', 'TX', 'SI', 'TB')
-LATEST = ('M1', 'S1', 'LX', 'N', 'QB', 'QW', 'WQ', 'TX', 'AD', 'QX', 'M0', 'N', 'SI', 'G1', 'MX', 'S0', 'LB', 'LA', 'SX', 'N', 'MF', 'G0', 'TB', 'W')
-TAIL = ('N', 'SI', 'LB', 'AD', 'N', 'MX', 'N', 'MF', 'LA', 'QB', 'N', 'TB')
+LS = 11
+SINGLES = 16
+LTX, LLX, LTB, LLB, LMA, LQX, LQB = 7, 6, 2, 3, 1, 4, 5
+STEP = ('SI', 'S1', 'WQ', 'SX', 'QW', 'S0', 'LX', 'AD', 'QX', 'M1', 'M0', 'LB', 'ZS', 'N', 'MF', 'N', 'QB', 'W', 'MX', 'TX', 'TB', 'G1', 'N', 'G0', 'LA')
+LATEST = ('MF', 'M0', 'WQ', 'S0', 'M1', 'S1', 'W', 'AD', 'N', 'LX', 'LA', 'G0', 'SI', 'ZS', 'QW', 'N', 'TX', 'MX', 'G1', 'TB', 'QX', 'N', 'SX', 'QB', 'LB')
+TAIL = ('N', 'LA', 'QB', 'MF', 'N', 'SI', 'ZS', 'LB', 'MX', 'N', 'AD', 'TB', 'N')
 
 
 def tile_autonomyofexpertsnormgate_t_kernel(tc, x_bytes, x_scale, wdown, rgain, wup, wp, out):
@@ -149,7 +149,7 @@ def tile_autonomyofexpertsnormgate_t_kernel(tc, x_bytes, x_scale, wdown, rgain, 
         xs, xt, xg, xc, xsc = {}, {}, {}, {}, {}
         acc, bb, bt, bg, bc, bsc = {}, {}, {}, {}, {}, {}
         ACCS = 8 - 2 - TURN[1] - (TURN[3] if TURN[0] != TURN[2] else 0)
-        pps, ups, sil = {}, {}, {}
+        pps, ups, sil, q, z = {}, {}, {}, {}, {}
         sumsq = keep.tile([P, TILES * E], F32, name="sumsq")
         gate = keep.tile([P, TILES, E], F32, name="gate")
 
@@ -293,24 +293,28 @@ def tile_autonomyofexpertsnormgate_t_kernel(tc, x_bytes, x_scale, wdown, rgain, 
             nc.scalar.activation(out=s_tile[:], in_=ups[k][:], func=ACT.Silu)
 
         def mix(k):
-            y = stage.tile([P, E, 2, F], F32, name="y", bufs=3)
+            q_tile = stage.tile([P, 2, E, F], F32, name="q", bufs=3)
+            q[k] = q_tile
+            nc.vector.tensor_tensor(
+                out=q_tile[:].rearrange("q m e f -> q (m e f)"),
+                in0=sil[k][:].rearrange("q m e f -> q (m e f)"),
+                in1=pps[k][:].rearrange("q m f -> q (m f)"),
+                op=ALU.mult,
+            )
+
+        def weigh(k):
+            z_tile = stage.tile([P, 2, F], F32, name="z", bufs=3)
+            z[k] = z_tile
+            for m in range(2):
+                nc.scalar.activation(out=z_tile[:, m, :], in_=q[k][:, m, 1, :], func=ACT.Copy, scale=gate[:, 2 * k + m, 1:2])
+
+        def join(k):
             o = stage.tile([P, 2, F], F32, name="o", bufs=3)
-            for e in range(E):
-                for m in range(2):
-                    nc.vector.scalar_tensor_tensor(
-                        out=y[:, e, m, :],
-                        in0=sil[k][:, m, e, :],
-                        scalar=gate[:, 2 * k + m, e : e + 1],
-                        in1=pps[k][:, m, e * F : (e + 1) * F],
-                        op0=ALU.mult,
-                        op1=ALU.mult,
-                    )
-
-            def add():
-                nc.vector.tensor_tensor(out=o[:], in0=y[:, 0], in1=y[:, 1], op=ALU.add)
-                nc.sync.dma_start(out=out[256 * k : 256 * k + 256, :].rearrange("(p m) f -> p m f", m=2), in_=o[:])
-
-            sums.append(add)
+            for m in range(2):
+                nc.vector.scalar_tensor_tensor(
+                    out=o[:, m, :], in0=q[k][:, m, 0, :], scalar=gate[:, 2 * k + m, 0:1], in1=z[k][:, m, :], op0=ALU.mult, op1=ALU.add
+                )
+            nc.sync.dma_start(out=out[256 * k : 256 * k + 256, :].rearrange("(p m) f -> p m f", m=2), in_=o[:])
 
         def gate_steps(first, count):
             t0, nt = 2 * first, 2 * count
@@ -352,6 +356,7 @@ def tile_autonomyofexpertsnormgate_t_kernel(tc, x_bytes, x_scale, wdown, rgain, 
             return [start] + [recip, divide, average] * 3 + [finish]
 
         silus = []
+        scales = []
         small = []
         ready = []
         final = []
@@ -398,10 +403,14 @@ def tile_autonomyofexpertsnormgate_t_kernel(tc, x_bytes, x_scale, wdown, rgain, 
                 elif tok == "N":
                     weave(1)
                 elif tok == "MX" and final:
-                    mix(final.pop(0))
+                    mix(final[0])
+                    scales.append(final[0])
+                    sums.append(final.pop(0))
                     done += 1
-                elif tok == "AD" and sums:
-                    sums.pop(0)()
+                elif tok == "ZS" and scales:
+                    weigh(scales.pop(0))
+                elif tok == "AD" and sums and sums[0] not in scales:
+                    join(sums.pop(0))
                 elif tok == "LA" and late and (s >= late[0][0] or s >= TILES):
                     late.pop(0)[1]()
                 elif tok == "QX" and (s + LQX) % 2 == 0 and 0 <= (s + LQX) // 2 < PAIRS:
@@ -438,5 +447,7 @@ def tile_autonomyofexpertsnormgate_t_kernel(tc, x_bytes, x_scale, wdown, rgain, 
             if waiting and waiting[0][0] <= s:
                 small.extend(gate_steps(*waiting.pop(0)[1]))
             s += 1
+        while scales:
+            weigh(scales.pop(0))
         while sums:
-            sums.pop(0)()
+            join(sums.pop(0))

from contextlib import ExitStack

import concourse.mybir as mybir
from concourse.masks import make_identity

T, D, E, R, F = 4096, 1024, 2, 512, 128
P = 128
PAIRS = T // (2 * P)
TILES = 2 * PAIRS
FLOPS = 2 * T * (D * E * R + D * E * F + E * R * F)

F32 = mybir.dt.float32
BF16 = mybir.dt.bfloat16
I32 = mybir.dt.int32
U32 = mybir.dt.uint32
U8 = mybir.dt.uint8
F8 = mybir.dt.float8_e4m3fn
X4 = mybir.dt.float8_e4m3fn_x4
ACT = mybir.ActivationFunctionType
ALU = mybir.AluOpType

SQRT_SEED = 532487669.0
GROUPS = (7, 4, 3, 2)
AHEAD = 9
PACE = 1.0
FLAG = 20
FEND = 73
WENG = 'vssssvss'
WPER = 2
WFROM = 2
WLAG = 2
TURN = ('xt', 2, 'xt', 2)
SEED = 0
LATE = 0
LS = 11
SINGLES = 16
LTX, LLX, LTB, LLB, LMA, LQX, LQB = 7, 6, 2, 3, 1, 4, 5
STEP = ('SI', 'S1', 'WQ', 'SX', 'QW', 'S0', 'LX', 'AD', 'QX', 'M1', 'M0', 'LB', 'ZS', 'N', 'MF', 'N', 'QB', 'W', 'MX', 'TX', 'TB', 'G1', 'N', 'G0', 'LA')
LATEST = ('MF', 'M0', 'WQ', 'S0', 'M1', 'S1', 'W', 'AD', 'N', 'LX', 'LA', 'G0', 'SI', 'ZS', 'QW', 'N', 'TX', 'MX', 'G1', 'TB', 'QX', 'N', 'SX', 'QB', 'LB')
TAIL = ('N', 'LA', 'QB', 'MF', 'N', 'SI', 'ZS', 'LB', 'MX', 'N', 'AD', 'TB', 'N')


def tile_autonomyofexpertsnormgate_t_kernel(tc, x_bytes, x_scale, wdown, rgain, wup, wp, out):
    nc = tc.nc
    with ExitStack() as ctx:
        keep = ctx.enter_context(tc.tile_pool(name="keep", bufs=1))
        stage = ctx.enter_context(tc.tile_pool(name="stage", bufs=2))
        psum = ctx.enter_context(tc.psum_pool(name="psum", bufs=1))
        ctx.enter_context(tc.manual_schedule())

        xscale = keep.tile([P, 2, D], F32, name="xscale")
        tiny = keep.tile([P, 1], F32, name="tiny")
        nc.vector.memset(tiny[:], 0.0)
        gain = keep.tile([P, E, 2 * P, 2], BF16, name="gain")

        xb = {}

        def load_x(k):
            xb_tile = stage.tile([P, 2, D], U8, name="xb", bufs=6)
            xb[k] = xb_tile
            nc.sync.dma_start(out=xb[k][:], in_=x_bytes[256 * k : 256 * k + 256, :].rearrange("(p m) d -> p m d", m=2))

        wraw, wcode, wscale = {}, {}, {}

        def load_w(e, g):
            w_tile = keep.tile([P, 4, R], BF16, name="wraw%d%d" % (e, g))
            wraw[e, g] = w_tile
            nc.sync.dma_start(out=w_tile[:], in_=wdown[e, 512 * g : 512 * g + 512, :].rearrange("(p j) c -> p j c", j=4))

        first = stage.tile([P, 2, D], U8, name="xb", bufs=6)
        xb[0] = first
        tokens = x_bytes[0:256, :].rearrange("(p m) d -> p m d", m=2)
        spread = x_scale.rearrange("o k -> (o k)")
        nc.sync.dma_start(out=xscale[:, 0, 0:512], in_=spread[0:512].partition_broadcast(P))
        nc.sync.dma_start(out=first[:, 0, :], in_=tokens[:, 0, :])
        nc.sync.dma_start(out=xscale[:, 0, 512:1024], in_=spread[512:1024].partition_broadcast(P))
        nc.sync.dma_start(out=first[:, 1, :], in_=tokens[:, 1, :])
        nc.scalar.activation(out=tiny[:], in_=tiny[:], func=ACT.Silu)
        nc.scalar.copy(out=xscale[:, 1, :], in_=xscale[:, 0, :])
        load_w(0, 0)
        load_x(1)
        load_w(0, 1)
        load_w(1, 0)
        load_x(2)
        load_w(1, 1)
        nc.scalar.dma_start(out=gain[:].rearrange("q e a i -> q (e a i)"), in_=rgain.rearrange("e r -> (e r)").partition_broadcast(P))
        load_x(3)
        praw = keep.tile([P, E, 2, 4, F], BF16, name="praw")
        for e in range(E):
            nc.sync.dma_start(out=praw[:, e], in_=wp[e].rearrange("(g p j) f -> p g j f", g=2, j=4))
        uraw = keep.tile([P, E, 4, F], BF16, name="uraw")
        nc.sync.dma_start(out=uraw[:], in_=wup.rearrange("e (p j) f -> p e j f", j=4))
        for k in range(4, PAIRS):
            load_x(k)

        ident = keep.tile([P, P], F32, name="ident")
        make_identity(nc, ident[:])

        wgrp = {}

        def group_w(eng, e, g, u):
            if u == 0:
                wg_tile = stage.tile([P, 4 * R], BF16, align_bytes=64, name="wgrp", bufs=2)
                wgrp[e, g] = wg_tile
            half = wgrp[e, g][:, 1024 * u : 1024 * (u + 1)].rearrange("q (i p j) -> q i p j", i=2, j=4)
            src = wraw[e, g][:].rearrange("q j (p t) -> q t p j", t=4)[:, 2 * u : 2 * u + 2]
            if eng == "s":
                nc.scalar.copy(out=half, in_=src)
            elif eng == "g":
                nc.gpsimd.tensor_copy(out=half, in_=src)
            else:
                nc.vector.tensor_copy(out=half, in_=src)

        def quant_w(e, g):
            c_tile = keep.tile([P, R], U32, align_bytes=64, name="wcode%d%d" % (e, g))
            s_tile = keep.tile([P, R], U8, align_bytes=64, name="wscale%d%d" % (e, g))
            wcode[e, g], wscale[e, g] = c_tile, s_tile
            nc.vector.quantize_mx(out=c_tile[:].bitcast(X4), scales=s_tile[:], in_=wgrp[e, g][:])

        pgrp = keep.tile([P, 2, 4 * E * F], BF16, align_bytes=64, name="pgrp")
        pcode = keep.tile([P, 2, E * F], U32, align_bytes=64, name="pcode")
        pscale = keep.tile([P, 2, E * F], U8, align_bytes=64, name="pscale")
        ugrp = keep.tile([P, 4 * E * F], BF16, align_bytes=64, name="ugrp")
        ucode = keep.tile([P, E * F], U32, align_bytes=64, name="ucode")
        uscale = keep.tile([P, E * F], U8, align_bytes=64, name="uscale")

        def group_p(g):
            nc.scalar.copy(
                out=pgrp[:, g, :].rearrange("q (e f j) -> q e f j", e=E, j=4),
                in_=praw[:, :, g].rearrange("q e j f -> q e f j"),
            )

        def quant_p(g):
            nc.vector.quantize_mx(out=pcode[:, g, :].bitcast(X4), scales=pscale[:, g, :], in_=pgrp[:, g, :])

        def group_u():
            nc.scalar.copy(
                out=ugrp[:].rearrange("q (e f j) -> q e f j", e=E, j=4),
                in_=uraw[:].rearrange("q e j f -> q e f j"),
            )

        def quant_u():
            nc.vector.quantize_mx(out=ucode[:].bitcast(X4), scales=uscale[:], in_=ugrp[:])

        sums = []
        clock = [0]
        late = []

        xs, xt, xg, xc, xsc = {}, {}, {}, {}, {}
        acc, bb, bt, bg, bc, bsc = {}, {}, {}, {}, {}, {}
        ACCS = 8 - 2 - TURN[1] - (TURN[3] if TURN[0] != TURN[2] else 0)
        pps, ups, sil, q, z = {}, {}, {}, {}, {}
        sumsq = keep.tile([P, TILES * E], F32, name="sumsq")
        gate = keep.tile([P, TILES, E], F32, name="gate")

        def scale_x(n):
            k, m = n // 2, n % 2
            if m == 0:
                xs_tile = stage.tile([P, 2, D], BF16, align_bytes=64, name="xs", bufs=AHEAD // 2 + 2)
                xs[k] = xs_tile
            if n == 0:
                for c in range(2):
                    cols = slice(512 * c, 512 * (c + 1))
                    nc.vector.tensor_tensor(out=xs[k][:, 0, cols], in0=xb[k][:, 0, cols].bitcast(F8), in1=xscale[:, 0, cols], op=ALU.mult)
                return 1
            if k < SINGLES:
                nc.vector.tensor_tensor(out=xs[k][:, m, :], in0=xb[k][:, m, :].bitcast(F8), in1=xscale[:, 0, :], op=ALU.mult)
                return 1
            nc.vector.tensor_tensor(
                out=xs[k][:].rearrange("q m d -> q (m d)"),
                in0=xb[k][:].rearrange("q m d -> q (m d)").bitcast(F8),
                in1=xscale[:].rearrange("q m d -> q (m d)"),
                op=ALU.mult,
            )
            return 2

        def turn_x(n):
            xt_tile = psum.tile([P, 2, 2, P], F32, name=TURN[0], bufs=TURN[1])
            xt[n] = xt_tile
            words = xs[n // 2][:, n % 2, :].bitcast(F32)
            for g in range(2):
                for u in range(2):
                    nc.tensor.transpose(xt_tile[:, g, u, :], words[:, 256 * g + u : 256 * (g + 1) : 2], ident[:])

        def leave_x(n):
            k, m = n // 2, n % 2
            if m == 0:
                xg_tile = stage.tile([P, 2 * D], BF16, align_bytes=64, name="xg", bufs=3)
                xg[k] = xg_tile
            nc.scalar.copy(
                out=xg[k][:, D * m : D * (m + 1)].bitcast(F32).rearrange("q (g r u) -> q g r u", g=2, u=2),
                in_=xt[n][:].rearrange("q g u r -> q g r u"),
            )

        def quant_x(k):
            c_tile = keep.tile([P, 4 * P], U32, align_bytes=64, name="xc%d" % k)
            s_tile = keep.tile([P, 4 * P], U8, align_bytes=64, name="xsc%d" % k)
            xc[k], xsc[k] = c_tile, s_tile
            nc.vector.quantize_mx(out=c_tile[:].bitcast(X4), scales=s_tile[:], in_=xg[k][:])

        def mm_a(n, e):
            k, m = n // 2, n % 2
            a_tile = psum.tile([P, R], F32, name="acc", bufs=ACCS)
            acc[n, e] = a_tile
            for g in range(2):
                cols = slice((2 * m + g) * P, (2 * m + g + 1) * P)
                nc.tensor.matmul_mx(
                    out=a_tile[:],
                    lhsT=xc[k][:, cols].bitcast(X4),
                    lhsT_scale=xsc[k][:, cols],
                    rhs=wcode[e, g][:].bitcast(X4),
                    rhs_scale=wscale[e, g][:],
                    start=(g == 0),
                    stop=(g == 1),
                )

        def gain_b(n, e):
            if n not in bb:
                bb_tile = stage.tile([P, E * R], BF16, align_bytes=64, name="bb", bufs=3)
                bb[n] = bb_tile
            nc.vector.tensor_tensor(
                out=bb[n][:, e * R : (e + 1) * R].rearrange("q (u p i) -> q u p i", u=2, i=2),
                in0=acc[n, e][:].rearrange("q (u i p) -> q u p i", u=2, i=2),
                in1=gain[:, e].rearrange("q (p u) i -> q u p i", u=2),
                op=ALU.mult,
            )

        def new_bg(k):
            if k not in bg:
                bg_tile = stage.tile([P, 2 * E * R], BF16, align_bytes=64, name="bg", bufs=3)
                bg[k] = bg_tile

        def square(n, e):
            junk = stage.tile([P, R], BF16, name="junk", bufs=2)
            nc.scalar.activation(out=junk[:], in_=acc[n, e][:], func=ACT.Square, accum_out=sumsq[:, 2 * n + e : 2 * n + e + 1])

        def turn_b(n):
            bt_tile = psum.tile([P, E, 2, P], F32, name=TURN[2], bufs=TURN[3])
            bt[n] = bt_tile
            words = bb[n][:].bitcast(F32)
            for e in range(E):
                for u in range(2):
                    nc.tensor.transpose(bt_tile[:, e, u, :], words[:, 256 * e + 128 * u : 256 * e + 128 * (u + 1)], ident[:])

        def leave_b(n):
            k, m = n // 2, n % 2
            ne = E
            new_bg(k)
            nc.scalar.copy(
                out=bg[k][:, E * R * m : E * R * m + ne * R].bitcast(F32).rearrange("q (e r u) -> q e r u", e=ne, u=2),
                in_=bt[n][:, 0:ne].rearrange("q e u r -> q e r u"),
            )

        def quant_b(k):
            c_tile = keep.tile([P, 4 * P], U32, align_bytes=64, name="bc%d" % k)
            s_tile = keep.tile([P, 4 * P], U8, align_bytes=64, name="bsc%d" % k)
            bc[k], bsc[k] = c_tile, s_tile
            nc.vector.quantize_mx(out=c_tile[:].bitcast(X4), scales=s_tile[:], in_=bg[k][:])

        def mm_final(k):
            p_tile = psum.tile([P, 2, E * F], F32, name="pp")
            u_tile = psum.tile([P, 2, E, F], F32, name="uu")
            pps[k], ups[k] = p_tile, u_tile
            for m in range(2):
                for e in range(E):
                    cols = slice((2 * m + e) * P, (2 * m + e + 1) * P)
                    ecols = slice(e * F, (e + 1) * F)
                    nc.tensor.matmul_mx(
                        out=u_tile[:, m, e, :],
                        lhsT=bc[k][:, cols].bitcast(X4),
                        lhsT_scale=bsc[k][:, cols],
                        rhs=ucode[:, ecols].bitcast(X4),
                        rhs_scale=uscale[:, ecols],
                        start=True,
                        stop=True,
                    )
            for m in range(2):
                for g in range(2):
                    cols = slice((2 * m + g) * P, (2 * m + g + 1) * P)
                    nc.tensor.matmul_mx(
                        out=p_tile[:, m, :],
                        lhsT=xc[k][:, cols].bitcast(X4),
                        lhsT_scale=xsc[k][:, cols],
                        rhs=pcode[:, g, :].bitcast(X4),
                        rhs_scale=pscale[:, g, :],
                        start=(g == 0),
                        stop=(g == 1),
                    )

        def silu(k):
            s_tile = stage.tile([P, 2, E, F], F32, name="sil", bufs=2)
            sil[k] = s_tile
            nc.scalar.activation(out=s_tile[:], in_=ups[k][:], func=ACT.Silu)

        def mix(k):
            q_tile = stage.tile([P, 2, E, F], F32, name="q", bufs=3)
            q[k] = q_tile
            nc.vector.tensor_tensor(
                out=q_tile[:].rearrange("q m e f -> q (m e f)"),
                in0=sil[k][:].rearrange("q m e f -> q (m e f)"),
                in1=pps[k][:].rearrange("q m f -> q (m f)"),
                op=ALU.mult,
            )

        def weigh(k):
            z_tile = stage.tile([P, 2, F], F32, name="z", bufs=3)
            z[k] = z_tile
            for m in range(2):
                nc.scalar.activation(out=z_tile[:, m, :], in_=q[k][:, m, 1, :], func=ACT.Copy, scale=gate[:, 2 * k + m, 1:2])

        def join(k):
            o = stage.tile([P, 2, F], F32, name="o", bufs=3)
            for m in range(2):
                nc.vector.scalar_tensor_tensor(
                    out=o[:, m, :], in0=q[k][:, m, 0, :], scalar=gate[:, 2 * k + m, 0:1], in1=z[k][:, m, :], op0=ALU.mult, op1=ALU.add
                )
            nc.sync.dma_start(out=out[256 * k : 256 * k + 256, :].rearrange("(p m) f -> p m f", m=2), in_=o[:])

        def gate_steps(first, count):
            t0, nt = 2 * first, 2 * count
            ss = sumsq[:, E * t0 : E * (t0 + nt)]
            seed = stage.tile([P, E * nt], I32, name="seed", bufs=2)
            state = {"y": seed[:].bitcast(F32)}

            def start():
                nc.vector.tensor_scalar(out=seed[:], in0=ss.bitcast(I32), scalar1=0.5, scalar2=SQRT_SEED, op0=ALU.mult, op1=ALU.add)

            def recip():
                r = stage.tile([P, E * nt], F32, name="newton_r", bufs=2)
                state["r"] = r
                nc.vector.reciprocal(out=r[:], in_=state["y"])

            def divide():
                t = stage.tile([P, E * nt], F32, name="newton_t", bufs=2)
                state["t"] = t
                nc.vector.scalar_tensor_tensor(out=t[:], in0=ss, scalar=0.5, in1=state["r"][:], op0=ALU.mult, op1=ALU.mult)

            def average():
                y = stage.tile([P, E * nt], F32, name="newton_y", bufs=2)
                nc.vector.scalar_tensor_tensor(out=y[:], in0=state["y"], scalar=0.5, in1=state["t"][:], op0=ALU.mult, op1=ALU.add)
                state["y"] = y[:]

            def finish():
                d = stage.tile([P, nt], F32, name="gate_d", bufs=2)
                h = stage.tile([P, nt], F32, name="gate_h", bufs=2)
                both = state["y"].rearrange("q (n e) -> q e n", e=E)
                nc.vector.tensor_tensor(out=d[:], in0=both[:, 0], in1=both[:, 1], op=ALU.subtract)
                late.append((clock[0] + LATE, lambda: squash(d, h)))

            def squash(d, h):
                nc.scalar.activation(out=h[:], in_=d[:], func=ACT.Tanh, scale=0.5)
                for e in range(E):
                    nc.scalar.activation(out=gate[:, t0 : t0 + nt, e], in_=h[:], func=ACT.Copy, scale=(0.5, -0.5)[e], bias=0.5)
                ready.extend(range(first, first + count))

            return [start] + [recip, divide, average] * 3 + [finish]

        silus = []
        scales = []
        small = []
        ready = []
        final = []
        bounds, total = {}, 0
        for count in GROUPS:
            bounds[2 * (total + count) - 1] = (total, count)
            total += count

        def weave(count):
            for i in range(count):
                if small:
                    small.pop(0)()

        done = 0
        s = -AHEAD
        waiting = []
        scaled = 0
        while done < PAIRS:
            clock[0] = s
            busy = 0 <= s < TILES
            for tok in (TAIL if s >= TILES else LATEST if s >= LS else STEP):
                if tok == "TX" and 0 <= s + LTX < TILES:
                    turn_x(s + LTX)
                elif tok == "LX" and 0 <= s + LLX < TILES:
                    leave_x(s + LLX)
                elif tok == "TB" and 0 <= s - LTB < TILES:
                    turn_b(s - LTB)
                elif tok == "LB" and 0 <= s - LLB < TILES:
                    leave_b(s - LLB)
                elif tok == "G0" and busy:
                    gain_b(s, 0)
                elif tok == "G1" and busy:
                    gain_b(s, 1)
                elif tok == "S0" and busy:
                    square(s, 0)
                elif tok == "S1" and busy:
                    square(s, 1)
                elif tok == "M0" and 0 <= s + LMA < TILES:
                    mm_a(s + LMA, 0)
                elif tok == "M1" and 0 <= s + LMA < TILES:
                    mm_a(s + LMA, 1)
                elif tok == "SX" and scaled < TILES and (scaled - AHEAD <= s if s < 0 else (scaled - AHEAD) * PACE <= s):
                    scaled += scale_x(scaled)
                elif tok == "N":
                    weave(1)
                elif tok == "MX" and final:
                    mix(final[0])
                    scales.append(final[0])
                    sums.append(final.pop(0))
                    done += 1
                elif tok == "ZS" and scales:
                    weigh(scales.pop(0))
                elif tok == "AD" and sums and sums[0] not in scales:
                    join(sums.pop(0))
                elif tok == "LA" and late and (s >= late[0][0] or s >= TILES):
                    late.pop(0)[1]()
                elif tok == "QX" and (s + LQX) % 2 == 0 and 0 <= (s + LQX) // 2 < PAIRS:
                    quant_x((s + LQX) // 2)
                elif tok == "QB" and (s - LQB) % 2 == 0 and 0 <= (s - LQB) // 2 < PAIRS:
                    quant_b((s - LQB) // 2)
                elif tok == "W":
                    for w in range(WPER * (s + AHEAD - WFROM), WPER * (s + AHEAD - WFROM + 1)):
                        if 0 <= w < 8:
                            group_w(WENG[w], w // 4, w // 2 % 2, w % 2)
                elif tok == "WQ":
                    for w in range(WPER * (s + AHEAD - WFROM - WLAG), WPER * (s + AHEAD - WFROM - WLAG + 1)):
                        if 0 <= w < 8 and w % 2 == 1:
                            quant_w(w // 4, w // 2 % 2)
                    if s in (1, 2):
                        group_p(s - 1)
                    if s == 3:
                        group_u()
                elif tok == "QW":
                    if s in (4, 5):
                        quant_p(s - 4)
                    if s == 6:
                        quant_u()
                elif tok == "MF":
                    if ready and ready[0] in bc and not final and (s >= 2 * ready[0] + FLAG or s >= TILES - FEND):
                        k = ready.pop(0)
                        mm_final(k)
                        final.append(k)
                        silus.append(k)
                elif tok == "SI" and silus:
                    silu(silus.pop(0))
            if s in bounds:
                waiting.append((s + SEED, bounds[s]))
            if waiting and waiting[0][0] <= s:
                small.extend(gate_steps(*waiting.pop(0)[1]))
            s += 1
        while scales:
            weigh(scales.pop(0))
        while sums:
            join(sums.pop(0))
